import numpy as np
import ml_dtypes


def mxq(x, axis, fmt="e4m3"):
    dtype, down = {"e4m3": (ml_dtypes.float8_e4m3fn, 7), "e5m2": (ml_dtypes.float8_e5m2, 14)}[fmt]
    v = np.moveaxis(np.asarray(x, np.float32).astype(ml_dtypes.bfloat16).astype(np.float64), axis, -1)
    blocks = v.reshape(v.shape[:-1] + (-1, 32))
    amax = np.abs(blocks).max(-1, keepdims=True)
    byte = np.maximum(np.where(amax > 0, np.frexp(amax)[1] - 1 + 127, 0) - down, 1)
    scale = np.exp2(byte - 127.0)
    codes = (blocks / scale).astype(np.float32).astype(dtype).astype(np.float64)
    return np.moveaxis((codes * scale).reshape(v.shape), -1, axis)


WIDE = False


def mx_kscale(k):
    if not WIDE:
        return np.ones(k)
    levels = np.array([10, -10, 5, -5, 0])
    if k % 512:
        return np.exp2(np.random.permutation(np.resize(levels, k // 32))).repeat(32)
    a = np.empty((k // 512, 16))
    for p in range(k // 512):
        a[p, :8] = np.random.permutation(np.resize(levels, 8))
        for g in range(8):
            far = levels[np.abs(levels - a[p, g]) >= 10]
            a[p, g + 8] = far[np.random.randint(len(far))]
    return np.exp2(a.ravel()).repeat(32)


def f64(x):
    return np.asarray(x).astype(np.float64)


def striped(idx):
    return np.tile(idx.reshape(-1, 16).T, (8, 1)).astype(np.uint16)


def unstriped(offs):
    return offs[:16].T.reshape(-1).astype(np.int64)


def pack_weight(w):
    k, n = w.shape
    w = f64(np.asarray(w, np.float32).astype(ml_dtypes.bfloat16)).reshape(k // 32, 32, n)
    amax = np.abs(w).max(1)
    byte = np.clip(np.where(amax > 0, np.frexp(amax)[1] - 1 + 127 - 7, 1), 1, 254)
    scaled = (w * np.exp2(127.0 - byte)[:, None, :]).reshape(k, n).astype(np.float32)
    words = np.ascontiguousarray(scaled.reshape(k // 512, 128, 4, n).transpose(0, 1, 3, 2)).astype(ml_dtypes.float8_e4m3fn).view(np.uint8)
    return words, np.ascontiguousarray(byte.astype(np.uint8).reshape(k // 512, 16, n))


def unpack_weight(words, scales):
    g, p, n, _ = words.shape
    vals = np.ascontiguousarray(words).view(ml_dtypes.float8_e4m3fn).astype(np.float64) * np.repeat(np.exp2(scales.astype(np.float64) - 127.0), 8, axis=1)[..., None]
    return vals.transpose(0, 1, 3, 2).reshape(g * 512, n)


def sigmoid(v):
    return 1.0 / (1.0 + np.exp(-np.maximum(v, -700.0)))

def planes(y):
    n, m = y.shape
    v = y.astype(np.float32).astype(ml_dtypes.bfloat16).astype(np.float64).reshape(n // 32, 32, m)
    top = np.abs(v).max(1)
    byte = np.clip(np.where(top > 0, np.frexp(top)[1] - 1 + 127 - 7, 1), 1, 254)
    codes = (v * np.exp2(127.0 - byte)[:, None, :]).reshape(n, m).astype(np.float32).astype(ml_dtypes.float8_e4m3fn).view(np.uint8)
    words = codes.reshape(n // 512, 128, 4, m).transpose(0, 1, 3, 2)
    return np.ascontiguousarray(words), np.ascontiguousarray(byte.astype(np.uint8).reshape(n // 512, 16, m))


K, T, S, N, H, W, U = 512, 2048, 512, 512, 512, 384, 256


def setup_inputs():
    n = np.random.standard_normal
    s = mx_kscale(K)[:, None]
    u = mx_kscale(H)
    packed_xT = pack_weight(n((K, T)) * s)
    packed_w1 = pack_weight(n((K, H)) / np.sqrt(K) / s)
    packed_w2 = pack_weight(n((H, N)) / np.sqrt(2 * H) / u[:, None])
    packed_w3 = pack_weight(n((K, N)) / np.sqrt(2 * K) / s)
    perm = np.random.permutation(S)
    return {
        "x_words": packed_xT[0],
        "x_scales": packed_xT[1],
        "w1_words": packed_w1[0],
        "w1_scales": packed_w1[1],
        "gn": (np.random.uniform(0.5, 1.5, (H, 1)) * u[:, None]).astype(np.float32),
        "w2_words": packed_w2[0],
        "w2_scales": packed_w2[1],
        "w3_words": packed_w3[0],
        "w3_scales": packed_w3[1],
        "offs": striped(np.random.permutation(T)[:S]),
        "n1": striped(np.random.permutation(S)[:W]),
        "n2": striped(np.random.permutation(S)[:W]),
        "two": striped(np.random.permutation(T)[:S]),
        "n3": striped(perm[:U]),
        "n4": striped(perm[U:]),
    }


def reference(x_words, x_scales, w1_words, w1_scales, gn, w2_words, w2_scales, w3_words, w3_scales, offs, n1, n2, two, n3, n4):
    xq = unpack_weight(x_words, x_scales)[:, unstriped(offs)]
    y = unpack_weight(w1_words, w1_scales).T @ xq
    old = y[:, unstriped(n1)]
    pa = y[:, unstriped(n2)]
    ra = old * sigmoid(pa)
    ds = y.copy()
    ds[:, unstriped(n1)] = ra
    z = f64(gn) * ds
    x_two = unpack_weight(x_words, x_scales)[:, unstriped(two)]
    h = unpack_weight(w2_words, w2_scales).T @ mxq(z, 0, "e4m3") + unpack_weight(w3_words, w3_scales).T @ x_two
    pa2 = h[:, unstriped(n3)]
    pb = h[:, unstriped(n4)]
    rb = np.maximum(0.5 * pa2, pb)
    ra2 = pb - pa2
    ds2 = np.zeros((N, S))
    ds2[:, unstriped(n3)] = ra2
    out = ds2.copy()
    out[:, unstriped(n4)] = rb
    return (out,) + planes(out)

@@ -1,0 +1,203 @@
+from contextlib import ExitStack
+
+import concourse.mybir as mybir
+
+K, T, S, N, H, W, U = 512, 2048, 512, 512, 512, 384, 256
+FLOPS = 3 * 2 * 512 * 512 * 512
+
+F32 = mybir.dt.float32
+BF16 = mybir.dt.bfloat16
+I32 = mybir.dt.int32
+U32 = mybir.dt.uint32
+U16 = mybir.dt.uint16
+U8 = mybir.dt.uint8
+FP8X4 = mybir.dt.float8_e4m3fn_x4
+ALU = mybir.AluOpType
+ACT = mybir.ActivationFunctionType
+
+P = 128
+PACK = 4
+
+
+def tile_picked_mixinkgatelift_none_po_kernel(
+    tc, x_words, x_scales, w1_words, w1_scales, gn, w2_words, w2_scales, w3_words, w3_scales,
+    offs, n1, n2, two, n3, n4, out_0, out_1, out_2,
+):
+    nc = tc.nc
+    with ExitStack() as ctx:
+        lists = ctx.enter_context(tc.tile_pool(name="lists", bufs=1))
+        keep = ctx.enter_context(tc.tile_pool(name="keep", bufs=1))
+        psum = ctx.enter_context(tc.psum_pool(name="psum", bufs=1))
+
+        def sb(name, shape, dtype):
+            return keep.tile(shape, dtype, name=name, align_bytes=64)
+
+        def load_list(name, src):
+            tile = lists.tile(list(src.shape), U16, name=name)
+            nc.sync.dma_start(tile[:], src)
+            return tile
+
+        def load_words(name, src, queue):
+            tile = sb(name, [P, src.shape[2]], U32)
+            queue.dma_start(tile[:].bitcast(I32), src[0].rearrange("p c r -> p (c r)").bitcast(I32))
+            return tile
+
+        def load_scales(tile, first, src, queue):
+            for q in range(4):
+                queue.dma_start(
+                    tile[32 * q + first : 32 * q + first + 4, :].bitcast(I32),
+                    src[0, 4 * q : 4 * q + 4, :].bitcast(I32),
+                )
+
+        def deal(name, src, dtype):
+            tile = sb(name, [P, 512], src.dtype)
+            nc.vector.tensor_copy(
+                tile[:].bitcast(dtype).rearrange("p (t m) -> p t m", t=PACK),
+                src[:].bitcast(dtype).rearrange("p (m t) -> p t m", t=PACK),
+            )
+            return tile
+
+        def gather_tokens(name, idx):
+            words = sb(name + "_words", [P, S], U32)
+            scales = sb(name + "_scales", [P, S], U8)
+            nc.vector.tensor_copy(scales[:], xs[:].indirect(idx[:]))
+            nc.vector.tensor_copy(words[:], xw[:].indirect(idx[:]))
+            return words, scales
+
+        def load_repeated(tile, src, q, queue):
+            rows = src[0, 4 * q : 4 * q + 4, :].bitcast(I32)
+            queue.dma_start(
+                tile[32 * q : 32 * q + 32, :].bitcast(I32),
+                rows.unsqueeze(0).to_broadcast([8, 4, rows.shape[1]]),
+            )
+
+        xs = sb("xs", [P, T], U8)
+        w1s_raw = sb("w1s_raw", [P, H], U8)
+        w23s_raw = sb("w23s_raw", [P, N], U8)
+        nc.vector.memset(w23s_raw[:].bitcast(I32), 0)
+
+        load_repeated(xs, x_scales, 0, nc.sync)
+        for q in range(1, 4):
+            load_repeated(xs, x_scales, q, nc.scalar)
+        offs_t = load_list("offs_t", offs)
+        load_repeated(w1s_raw, w1_scales, 0, nc.sync)
+        xw = load_words("xw", x_words, nc.sync)
+        w1_raw = load_words("w1_raw", w1_words, nc.scalar)
+        load_repeated(w1s_raw, w1_scales, 1, nc.sync)
+        load_repeated(w1s_raw, w1_scales, 2, nc.scalar)
+        load_repeated(w1s_raw, w1_scales, 3, nc.scalar)
+        two_t = load_list("two_t", two)
+        n2_t = load_list("n2_t", n2)
+        n1_t = load_list("n1_t", n1)
+        w3_raw = load_words("w3_raw", w3_words, nc.sync)
+        w2_raw = load_words("w2_raw", w2_words, nc.sync)
+        load_scales(w23s_raw, 0, w2_scales, nc.sync)
+        load_scales(w23s_raw, 4, w3_scales, nc.sync)
+        gn_t = sb("gn_t", [P, PACK], F32)
+        nc.sync.dma_start(gn_t[:], gn.rearrange("(p t) o -> p (t o)", t=PACK))
+        n3_t = load_list("n3_t", n3)
+        n4_t = load_list("n4_t", n4)
+
+        w1 = deal("w1", w1_raw, I32)
+        w1s = deal("w1s", w1s_raw, U8)
+        xa, xa_s = gather_tokens("xa", offs_t)
+
+        y_ps = [psum.tile([P, S], F32, name=f"y_ps{t}") for t in range(PACK)]
+        h_ps = [psum.tile([P, S], F32, name=f"h_ps{t}") for t in range(PACK)]
+        for t in range(PACK):
+            cols = slice(t * P, (t + 1) * P)
+            nc.tensor.matmul_mx(
+                out=y_ps[t][:], lhsT=w1[:, cols].bitcast(FP8X4), lhsT_scale=w1s[:, cols],
+                rhs=xa[:].bitcast(FP8X4), rhs_scale=xa_s[:], start=True, stop=True,
+            )
+        xb, xb_s = gather_tokens("xb", two_t)
+
+        def quantise(name, pairs):
+            grouped = sb(name + "_grouped", [P, S, 2], I32)
+            nc.vector.tensor_copy(
+                grouped[:], pairs[:].rearrange("p u c e -> p u (c e)").bitcast(I32).rearrange("p u c -> p c u")
+            )
+            words = sb(name + "_words", [P, S], U32)
+            scales = sb(name + "_scales", [P, S], U8)
+            nc.vector.quantize_mx(
+                out=words[:].bitcast(FP8X4), scales=scales[:],
+                in_=grouped[:].rearrange("p c u -> p (c u)").bitcast(BF16),
+            )
+            return words, scales
+
+        ys = [sb(f"y{t}", [P, S], F32) for t in range(PACK)]
+        gates = [sb(f"gate{t}", [P, W], F32) for t in range(PACK)]
+        olds = [sb(f"old{t}", [P, W], F32) for t in range(PACK)]
+        z_pairs = sb("z_pairs", [P, 2, S, 2], BF16)
+        half = W // 2
+        for t in range(PACK):
+            nc.scalar.copy(ys[t][:], y_ps[t][:])
+            for i in range(2):
+                nc.scalar.activation(
+                    gates[t][:, i * half : (i + 1) * half],
+                    ys[t][:].indirect(n2_t[:, i * half // 16 : (i + 1) * half // 16]),
+                    ACT.Sigmoid,
+                )
+
+        def mix_vector(t):
+            nc.vector.tensor_copy(olds[t][:], ys[t][:].indirect(n1_t[:]))
+            nc.vector.tensor_tensor(ys[t][:].indirect(n1_t[:]), olds[t][:], gates[t][:], ALU.mult)
+
+        def mix_scalar(t):
+            nc.vector.tensor_tensor(olds[t][:], ys[t][:].indirect(n1_t[:]), gates[t][:], ALU.mult)
+            nc.scalar.activation(ys[t][:].indirect(n1_t[:]), olds[t][:], ACT.Copy)
+
+        def round_z(t):
+            nc.vector.tensor_scalar(
+                z_pairs[:, t // 2, :, t % 2], ys[t][:], gn_t[:, t : t + 1], None, ALU.mult
+            )
+
+        mix_scalar(0)
+        mix_scalar(1)
+        mix_vector(2)
+        mix_vector(3)
+        w3 = deal("w3", w3_raw, I32)
+        w2 = deal("w2", w2_raw, I32)
+        w23s = deal("w23s", w23s_raw, U8)
+        for t in range(PACK):
+            cols = slice(t * P, (t + 1) * P)
+            nc.tensor.matmul_mx(
+                out=h_ps[t][:], lhsT=w3[:, cols].bitcast(FP8X4), lhsT_scale=w23s[4:P, cols],
+                rhs=xb[:].bitcast(FP8X4), rhs_scale=xb_s[:], start=True, stop=False,
+            )
+        for t in (2, 3, 0, 1):
+            round_z(t)
+        zq, zq_s = quantise("z", z_pairs)
+        for t in range(PACK):
+            cols = slice(t * P, (t + 1) * P)
+            nc.tensor.matmul_mx(
+                out=h_ps[t][:], lhsT=w2[:, cols].bitcast(FP8X4), lhsT_scale=w23s[:, cols],
+                rhs=zq[:].bitcast(FP8X4), rhs_scale=zq_s[:], start=False, stop=True,
+            )
+
+        out_rows = out_0.rearrange("(p t) c -> t p c", t=PACK)
+        o_pairs = sb("o_pairs", [P, 2, S, 2], BF16)
+        outs = [sb(f"o{t}", [P, S], F32) for t in range(PACK)]
+        tops = [sb(f"top{t}", [P, U], F32) for t in range(PACK)]
+        for t in range(PACK):
+            h = sb(f"h{t}", [P, S], F32)
+            neg_a = sb(f"neg_a{t}", [P, U], F32)
+            b = sb(f"b{t}", [P, U], F32)
+            nc.scalar.copy(h[:], h_ps[t][:])
+            nc.scalar.activation(neg_a[:], h[:].indirect(n3_t[:]), ACT.Copy, scale=-1.0)
+            if t == 1:
+                nc.scalar.activation(b[:], h[:].indirect(n4_t[:]), ACT.Copy)
+            else:
+                nc.vector.tensor_copy(b[:], h[:].indirect(n4_t[:]))
+            nc.vector.scalar_tensor_tensor(tops[t][:], neg_a[:], -0.5, b[:], ALU.mult, ALU.max)
+            nc.vector.tensor_tensor(outs[t][:].indirect(n3_t[:]), b[:], neg_a[:], ALU.add)
+        for t in range(PACK):
+            nc.scalar.activation(outs[t][:].indirect(n4_t[:]), tops[t][:], ACT.Copy)
+            nc.sync.dma_start(out_rows[t], outs[t][:])
+        for t in range(PACK):
+            nc.vector.tensor_copy(o_pairs[:, t // 2, :, t % 2], outs[t][:])
+        oq, oq_s = quantise("o", o_pairs)
+        nc.sync.dma_start(out_1[0].rearrange("p c r -> p (c r)").bitcast(I32), oq[:].bitcast(I32))
+        for q in range(4):
+            queue = nc.sync if q % 2 == 0 else nc.scalar
+            queue.dma_start(out_2[0, 4 * q : 4 * q + 4, :].bitcast(I32), oq_s[32 * q : 32 * q + 4, :].bitcast(I32))

@@ -17,6 +17,8 @@ ACT = mybir.ActivationFunctionType
 
 P = 128
 PACK = 4
+HALF = S // 2
+ORDER = (0, 2, 1, 3)
 
 
 def tile_picked_mixinkgatelift_none_po_kernel(
@@ -29,16 +31,16 @@ def tile_picked_mixinkgatelift_none_po_kernel(
         keep = ctx.enter_context(tc.tile_pool(name="keep", bufs=1))
         psum = ctx.enter_context(tc.psum_pool(name="psum", bufs=1))
 
-        def sb(name, shape, dtype):
-            return keep.tile(shape, dtype, name=name, align_bytes=64)
+        def sb(name, shape, dtype, tag=None):
+            return keep.tile(shape, dtype, name=name, tag=tag or name, align_bytes=64)
 
         def load_list(name, src):
             tile = lists.tile(list(src.shape), U16, name=name)
             nc.sync.dma_start(tile[:], src)
             return tile
 
-        def load_words(name, src, queue):
-            tile = sb(name, [P, src.shape[2]], U32)
+        def load_words(name, src, queue, tag=None):
+            tile = sb(name, [P, src.shape[2]], U32, tag)
             queue.dma_start(tile[:].bitcast(I32), src[0].rearrange("p c r -> p (c r)").bitcast(I32))
             return tile
 
@@ -50,15 +52,16 @@ def tile_picked_mixinkgatelift_none_po_kernel(
                 )
 
         def deal(name, src, dtype):
+            run = 4 if dtype == I32 else 16
             tile = sb(name, [P, 512], src.dtype)
             nc.vector.tensor_copy(
-                tile[:].bitcast(dtype).rearrange("p (t m) -> p t m", t=PACK),
-                src[:].bitcast(dtype).rearrange("p (m t) -> p t m", t=PACK),
+                tile[:].bitcast(dtype).rearrange("p (t b m) -> p b t m", t=PACK, m=run),
+                src[:].bitcast(dtype).rearrange("p (b m t) -> p b t m", t=PACK, m=run),
             )
             return tile
 
-        def gather_tokens(name, idx):
-            words = sb(name + "_words", [P, S], U32)
+        def gather_tokens(name, idx, tag=None):
+            words = sb(name + "_words", [P, S], U32, tag)
             scales = sb(name + "_scales", [P, S], U8)
             nc.vector.tensor_copy(scales[:], xs[:].indirect(idx[:]))
             nc.vector.tensor_copy(words[:], xw[:].indirect(idx[:]))
@@ -76,17 +79,14 @@ def tile_picked_mixinkgatelift_none_po_kernel(
         w23s_raw = sb("w23s_raw", [P, N], U8)
         nc.vector.memset(w23s_raw[:].bitcast(I32), 0)
 
-        load_repeated(xs, x_scales, 0, nc.sync)
-        for q in range(1, 4):
-            load_repeated(xs, x_scales, q, nc.scalar)
+        for q in range(4):
+            load_repeated(xs, x_scales, q, nc.sync if q == 0 else nc.scalar)
         offs_t = load_list("offs_t", offs)
-        load_repeated(w1s_raw, w1_scales, 0, nc.sync)
-        xw = load_words("xw", x_words, nc.sync)
-        w1_raw = load_words("w1_raw", w1_words, nc.scalar)
-        load_repeated(w1s_raw, w1_scales, 1, nc.sync)
-        load_repeated(w1s_raw, w1_scales, 2, nc.scalar)
-        load_repeated(w1s_raw, w1_scales, 3, nc.scalar)
         two_t = load_list("two_t", two)
+        xw = load_words("xw", x_words, nc.sync)
+        for q in range(4):
+            load_repeated(w1s_raw, w1_scales, q, nc.scalar if q % 2 == 0 else nc.sync)
+        w1_raw = load_words("w1_raw", w1_words, nc.scalar, "w1_raw_then_xb")
         n2_t = load_list("n2_t", n2)
         n1_t = load_list("n1_t", n1)
         w3_raw = load_words("w3_raw", w3_words, nc.sync)
@@ -104,58 +104,64 @@ def tile_picked_mixinkgatelift_none_po_kernel(
 
         y_ps = [psum.tile([P, S], F32, name=f"y_ps{t}") for t in range(PACK)]
         h_ps = [psum.tile([P, S], F32, name=f"h_ps{t}") for t in range(PACK)]
-        for t in range(PACK):
+        for t in ORDER:
             cols = slice(t * P, (t + 1) * P)
             nc.tensor.matmul_mx(
                 out=y_ps[t][:], lhsT=w1[:, cols].bitcast(FP8X4), lhsT_scale=w1s[:, cols],
                 rhs=xa[:].bitcast(FP8X4), rhs_scale=xa_s[:], start=True, stop=True,
             )
-        xb, xb_s = gather_tokens("xb", two_t)
+        xb, xb_s = gather_tokens("xb", two_t, "w1_raw_then_xb")
+
+        def pair_tiles(name):
+            return [sb(f"{name}_pairs{i}", [P, 2, HALF, 2], BF16) for i in range(2)]
+
+        def round_rows(engine, pairs, t, src, scale):
+            for i in range(2):
+                dst = pairs[i][:, t // 2, :, t % 2]
+                cols = src[:, i * HALF : (i + 1) * HALF]
+                if engine is nc.scalar:
+                    nc.scalar.activation(dst, cols, ACT.Copy, scale=scale)
+                else:
+                    nc.vector.tensor_scalar(dst, cols, scale, None, ALU.mult)
 
         def quantise(name, pairs):
-            grouped = sb(name + "_grouped", [P, S, 2], I32)
-            nc.vector.tensor_copy(
-                grouped[:], pairs[:].rearrange("p u c e -> p u (c e)").bitcast(I32).rearrange("p u c -> p c u")
-            )
-            words = sb(name + "_words", [P, S], U32)
+            grouped = [sb(f"{name}_grouped{i}", [P, HALF, 2], I32) for i in range(2)]
+            words = [sb(f"{name}_words{i}", [P, HALF], U32) for i in range(2)]
             scales = sb(name + "_scales", [P, S], U8)
-            nc.vector.quantize_mx(
-                out=words[:].bitcast(FP8X4), scales=scales[:],
-                in_=grouped[:].rearrange("p c u -> p (c u)").bitcast(BF16),
-            )
+            for i in range(2):
+                nc.vector.tensor_copy(
+                    grouped[i][:],
+                    pairs[i][:].rearrange("p u c e -> p u (c e)").bitcast(I32).rearrange("p u c -> p c u"),
+                )
+            for i in range(2):
+                nc.vector.quantize_mx(
+                    out=words[i][:].bitcast(FP8X4), scales=scales[:, i * HALF : (i + 1) * HALF],
+                    in_=grouped[i][:].rearrange("p c u -> p (c u)").bitcast(BF16),
+                )
             return words, scales
 
         ys = [sb(f"y{t}", [P, S], F32) for t in range(PACK)]
         gates = [sb(f"gate{t}", [P, W], F32) for t in range(PACK)]
         olds = [sb(f"old{t}", [P, W], F32) for t in range(PACK)]
-        z_pairs = sb("z_pairs", [P, 2, S, 2], BF16)
-        half = W // 2
-        for t in range(PACK):
+        z_pairs = pair_tiles("z")
+        part = W // 2
+        for t in ORDER:
             nc.scalar.copy(ys[t][:], y_ps[t][:])
             for i in range(2):
                 nc.scalar.activation(
-                    gates[t][:, i * half : (i + 1) * half],
-                    ys[t][:].indirect(n2_t[:, i * half // 16 : (i + 1) * half // 16]),
+                    gates[t][:, i * part : (i + 1) * part],
+                    ys[t][:].indirect(n2_t[:, i * part // 16 : (i + 1) * part // 16]),
                     ACT.Sigmoid,
                 )
 
-        def mix_vector(t):
-            nc.vector.tensor_copy(olds[t][:], ys[t][:].indirect(n1_t[:]))
-            nc.vector.tensor_tensor(ys[t][:].indirect(n1_t[:]), olds[t][:], gates[t][:], ALU.mult)
+        for t in ORDER:
+            if t < 2:
+                nc.vector.tensor_tensor(olds[t][:], ys[t][:].indirect(n1_t[:]), gates[t][:], ALU.mult)
+                nc.scalar.activation(ys[t][:].indirect(n1_t[:]), olds[t][:], ACT.Copy)
+            else:
+                nc.vector.tensor_copy(olds[t][:], ys[t][:].indirect(n1_t[:]))
+                nc.vector.tensor_tensor(ys[t][:].indirect(n1_t[:]), olds[t][:], gates[t][:], ALU.mult)
 
-        def mix_scalar(t):
-            nc.vector.tensor_tensor(olds[t][:], ys[t][:].indirect(n1_t[:]), gates[t][:], ALU.mult)
-            nc.scalar.activation(ys[t][:].indirect(n1_t[:]), olds[t][:], ACT.Copy)
-
-        def round_z(t):
-            nc.vector.tensor_scalar(
-                z_pairs[:, t // 2, :, t % 2], ys[t][:], gn_t[:, t : t + 1], None, ALU.mult
-            )
-
-        mix_scalar(0)
-        mix_scalar(1)
-        mix_vector(2)
-        mix_vector(3)
         w3 = deal("w3", w3_raw, I32)
         w2 = deal("w2", w2_raw, I32)
         w23s = deal("w23s", w23s_raw, U8)
@@ -165,18 +171,20 @@ def tile_picked_mixinkgatelift_none_po_kernel(
                 out=h_ps[t][:], lhsT=w3[:, cols].bitcast(FP8X4), lhsT_scale=w23s[4:P, cols],
                 rhs=xb[:].bitcast(FP8X4), rhs_scale=xb_s[:], start=True, stop=False,
             )
-        for t in (2, 3, 0, 1):
-            round_z(t)
+        for t in ORDER:
+            round_rows(nc.scalar if t < 2 else nc.vector, z_pairs, t, ys[t], gn_t[:, t : t + 1])
         zq, zq_s = quantise("z", z_pairs)
         for t in range(PACK):
             cols = slice(t * P, (t + 1) * P)
-            nc.tensor.matmul_mx(
-                out=h_ps[t][:], lhsT=w2[:, cols].bitcast(FP8X4), lhsT_scale=w23s[:, cols],
-                rhs=zq[:].bitcast(FP8X4), rhs_scale=zq_s[:], start=False, stop=True,
-            )
+            for i in range(2):
+                side = slice(i * HALF, (i + 1) * HALF)
+                nc.tensor.matmul_mx(
+                    out=h_ps[t][:, side], lhsT=w2[:, cols].bitcast(FP8X4), lhsT_scale=w23s[:, cols],
+                    rhs=zq[i][:].bitcast(FP8X4), rhs_scale=zq_s[:, side], start=False, stop=(i == 1),
+                )
 
         out_rows = out_0.rearrange("(p t) c -> t p c", t=PACK)
-        o_pairs = sb("o_pairs", [P, 2, S, 2], BF16)
+        o_pairs = pair_tiles("o")
         outs = [sb(f"o{t}", [P, S], F32) for t in range(PACK)]
         tops = [sb(f"top{t}", [P, U], F32) for t in range(PACK)]
         for t in range(PACK):
@@ -185,19 +193,24 @@ def tile_picked_mixinkgatelift_none_po_kernel(
             b = sb(f"b{t}", [P, U], F32)
             nc.scalar.copy(h[:], h_ps[t][:])
             nc.scalar.activation(neg_a[:], h[:].indirect(n3_t[:]), ACT.Copy, scale=-1.0)
-            if t == 1:
+            if t >= 2:
                 nc.scalar.activation(b[:], h[:].indirect(n4_t[:]), ACT.Copy)
             else:
                 nc.vector.tensor_copy(b[:], h[:].indirect(n4_t[:]))
             nc.vector.scalar_tensor_tensor(tops[t][:], neg_a[:], -0.5, b[:], ALU.mult, ALU.max)
             nc.vector.tensor_tensor(outs[t][:].indirect(n3_t[:]), b[:], neg_a[:], ALU.add)
         for t in range(PACK):
-            nc.scalar.activation(outs[t][:].indirect(n4_t[:]), tops[t][:], ACT.Copy)
+            if t < 3:
+                nc.scalar.activation(outs[t][:].indirect(n4_t[:]), tops[t][:], ACT.Copy)
+            else:
+                nc.vector.tensor_copy(outs[t][:].indirect(n4_t[:]), tops[t][:])
             nc.sync.dma_start(out_rows[t], outs[t][:])
         for t in range(PACK):
-            nc.vector.tensor_copy(o_pairs[:, t // 2, :, t % 2], outs[t][:])
+            round_rows(nc.scalar if t < 2 else nc.vector, o_pairs, t, outs[t], 1.0)
         oq, oq_s = quantise("o", o_pairs)
-        nc.sync.dma_start(out_1[0].rearrange("p c r -> p (c r)").bitcast(I32), oq[:].bitcast(I32))
+        words_out = out_1[0].rearrange("p c r -> p (c r)").bitcast(I32)
+        for i in range(2):
+            nc.sync.dma_start(words_out[:, i * HALF : (i + 1) * HALF], oq[i][:].bitcast(I32))
         for q in range(4):
-            queue = nc.sync if q % 2 == 0 else nc.scalar
+            queue = nc.scalar if q % 2 == 0 else nc.sync
             queue.dma_start(out_2[0, 4 * q : 4 * q + 4, :].bitcast(I32), oq_s[32 * q : 32 * q + 4, :].bitcast(I32))

@@ -18,7 +18,7 @@ ACT = mybir.ActivationFunctionType
 P = 128
 PACK = 4
 HALF = S // 2
-ORDER = (0, 2, 1, 3)
+ORDER = (0, 1, 2, 3)
 
 
 def tile_picked_mixinkgatelift_none_po_kernel(
@@ -51,9 +51,9 @@ def tile_picked_mixinkgatelift_none_po_kernel(
                     src[0, 4 * q : 4 * q + 4, :].bitcast(I32),
                 )
 
-        def deal(name, src, dtype):
+        def deal(name, src, dtype, tag=None):
             run = 4 if dtype == I32 else 16
-            tile = sb(name, [P, 512], src.dtype)
+            tile = sb(name, [P, 512], src.dtype, tag)
             nc.vector.tensor_copy(
                 tile[:].bitcast(dtype).rearrange("p (t b m) -> p b t m", t=PACK, m=run),
                 src[:].bitcast(dtype).rearrange("p (b m t) -> p b t m", t=PACK, m=run),
@@ -75,7 +75,7 @@ def tile_picked_mixinkgatelift_none_po_kernel(
             )
 
         xs = sb("xs", [P, T], U8)
-        w1s_raw = sb("w1s_raw", [P, H], U8)
+        w1s_raw = sb("w1s_raw", [P, H], U8, "w1s_raw_then_w1")
         w23s_raw = sb("w23s_raw", [P, N], U8)
         nc.vector.memset(w23s_raw[:].bitcast(I32), 0)
 
@@ -85,8 +85,8 @@ def tile_picked_mixinkgatelift_none_po_kernel(
         two_t = load_list("two_t", two)
         xw = load_words("xw", x_words, nc.sync)
         for q in range(4):
-            load_repeated(w1s_raw, w1_scales, q, nc.scalar if q % 2 == 0 else nc.sync)
-        w1_raw = load_words("w1_raw", w1_words, nc.scalar, "w1_raw_then_xb")
+            load_repeated(w1s_raw, w1_scales, q, nc.sync)
+        w1_raw = load_words("w1_raw", w1_words, nc.sync, "w1_raw_then_xb")
         n2_t = load_list("n2_t", n2)
         n1_t = load_list("n1_t", n1)
         w3_raw = load_words("w3_raw", w3_words, nc.sync)
@@ -98,9 +98,13 @@ def tile_picked_mixinkgatelift_none_po_kernel(
         n3_t = load_list("n3_t", n3)
         n4_t = load_list("n4_t", n4)
 
-        w1 = deal("w1", w1_raw, I32)
-        w1s = deal("w1s", w1s_raw, U8)
         xa, xa_s = gather_tokens("xa", offs_t)
+        w1s = deal("w1s", w1s_raw, U8)
+        w1 = deal("w1", w1_raw, I32, "w1s_raw_then_w1")
+        warm = sb("warm", [P, 1], F32)
+        warm2 = sb("warm2", [P, 1], F32)
+        nc.vector.memset(warm[:], 0.0)
+        nc.scalar.activation(warm2[:], warm[:], ACT.Sigmoid)
 
         y_ps = [psum.tile([P, S], F32, name=f"y_ps{t}") for t in range(PACK)]
         h_ps = [psum.tile([P, S], F32, name=f"h_ps{t}") for t in range(PACK)]
@@ -126,7 +130,7 @@ def tile_picked_mixinkgatelift_none_po_kernel(
 
         def quantise(name, pairs):
             grouped = [sb(f"{name}_grouped{i}", [P, HALF, 2], I32) for i in range(2)]
-            words = [sb(f"{name}_words{i}", [P, HALF], U32) for i in range(2)]
+            words = sb(name + "_words", [P, S], U32)
             scales = sb(name + "_scales", [P, S], U8)
             for i in range(2):
                 nc.vector.tensor_copy(
@@ -135,7 +139,7 @@ def tile_picked_mixinkgatelift_none_po_kernel(
                 )
             for i in range(2):
                 nc.vector.quantize_mx(
-                    out=words[i][:].bitcast(FP8X4), scales=scales[:, i * HALF : (i + 1) * HALF],
+                    out=words[:, i * HALF : (i + 1) * HALF].bitcast(FP8X4), scales=scales[:, i * HALF : (i + 1) * HALF],
                     in_=grouped[i][:].rearrange("p c u -> p (c u)").bitcast(BF16),
                 )
             return words, scales
@@ -146,20 +150,25 @@ def tile_picked_mixinkgatelift_none_po_kernel(
         z_pairs = pair_tiles("z")
         part = W // 2
         for t in ORDER:
-            nc.scalar.copy(ys[t][:], y_ps[t][:])
+            if t == 3:
+                nc.vector.tensor_copy(ys[t][:], y_ps[t][:])
+            else:
+                nc.scalar.copy(ys[t][:], y_ps[t][:])
             for i in range(2):
                 nc.scalar.activation(
                     gates[t][:, i * part : (i + 1) * part],
                     ys[t][:].indirect(n2_t[:, i * part // 16 : (i + 1) * part // 16]),
                     ACT.Sigmoid,
                 )
+        nc.scalar.activation(olds[3][:], ys[3][:].indirect(n1_t[:]), ACT.Copy)
 
         for t in ORDER:
-            if t < 2:
+            if t in (1, 2):
                 nc.vector.tensor_tensor(olds[t][:], ys[t][:].indirect(n1_t[:]), gates[t][:], ALU.mult)
                 nc.scalar.activation(ys[t][:].indirect(n1_t[:]), olds[t][:], ACT.Copy)
             else:
-                nc.vector.tensor_copy(olds[t][:], ys[t][:].indirect(n1_t[:]))
+                if t == 0:
+                    nc.vector.tensor_copy(olds[t][:], ys[t][:].indirect(n1_t[:]))
                 nc.vector.tensor_tensor(ys[t][:].indirect(n1_t[:]), olds[t][:], gates[t][:], ALU.mult)
 
         w3 = deal("w3", w3_raw, I32)
@@ -172,15 +181,15 @@ def tile_picked_mixinkgatelift_none_po_kernel(
                 rhs=xb[:].bitcast(FP8X4), rhs_scale=xb_s[:], start=True, stop=False,
             )
         for t in ORDER:
-            round_rows(nc.scalar if t < 2 else nc.vector, z_pairs, t, ys[t], gn_t[:, t : t + 1])
+            round_rows(nc.vector, z_pairs, t, ys[t], gn_t[:, t : t + 1])
         zq, zq_s = quantise("z", z_pairs)
         for t in range(PACK):
             cols = slice(t * P, (t + 1) * P)
-            for i in range(2):
-                side = slice(i * HALF, (i + 1) * HALF)
+            sides = [slice(0, HALF), slice(HALF, S)] if t == 0 else [slice(0, S)]
+            for side in sides:
                 nc.tensor.matmul_mx(
                     out=h_ps[t][:, side], lhsT=w2[:, cols].bitcast(FP8X4), lhsT_scale=w23s[:, cols],
-                    rhs=zq[i][:].bitcast(FP8X4), rhs_scale=zq_s[:, side], start=False, stop=(i == 1),
+                    rhs=zq[:, side].bitcast(FP8X4), rhs_scale=zq_s[:, side], start=False, stop=(side.stop == S),
                 )
 
         out_rows = out_0.rearrange("(p t) c -> t p c", t=PACK)
@@ -191,7 +200,10 @@ def tile_picked_mixinkgatelift_none_po_kernel(
             h = sb(f"h{t}", [P, S], F32)
             neg_a = sb(f"neg_a{t}", [P, U], F32)
             b = sb(f"b{t}", [P, U], F32)
-            nc.scalar.copy(h[:], h_ps[t][:])
+            if t == 1:
+                nc.vector.tensor_copy(h[:], h_ps[t][:])
+            else:
+                nc.scalar.copy(h[:], h_ps[t][:])
             nc.scalar.activation(neg_a[:], h[:].indirect(n3_t[:]), ACT.Copy, scale=-1.0)
             if t >= 2:
                 nc.scalar.activation(b[:], h[:].indirect(n4_t[:]), ACT.Copy)
@@ -200,17 +212,14 @@ def tile_picked_mixinkgatelift_none_po_kernel(
             nc.vector.scalar_tensor_tensor(tops[t][:], neg_a[:], -0.5, b[:], ALU.mult, ALU.max)
             nc.vector.tensor_tensor(outs[t][:].indirect(n3_t[:]), b[:], neg_a[:], ALU.add)
         for t in range(PACK):
-            if t < 3:
-                nc.scalar.activation(outs[t][:].indirect(n4_t[:]), tops[t][:], ACT.Copy)
-            else:
-                nc.vector.tensor_copy(outs[t][:].indirect(n4_t[:]), tops[t][:])
+            nc.scalar.activation(outs[t][:].indirect(n4_t[:]), tops[t][:], ACT.Copy)
             nc.sync.dma_start(out_rows[t], outs[t][:])
         for t in range(PACK):
-            round_rows(nc.scalar if t < 2 else nc.vector, o_pairs, t, outs[t], 1.0)
+            round_rows(nc.vector, o_pairs, t, outs[t], 1.0)
         oq, oq_s = quantise("o", o_pairs)
         words_out = out_1[0].rearrange("p c r -> p (c r)").bitcast(I32)
         for i in range(2):
-            nc.sync.dma_start(words_out[:, i * HALF : (i + 1) * HALF], oq[i][:].bitcast(I32))
+            nc.sync.dma_start(words_out[:, i * HALF : (i + 1) * HALF], oq[:, i * HALF : (i + 1) * HALF].bitcast(I32))
         for q in range(4):
             queue = nc.scalar if q % 2 == 0 else nc.sync
             queue.dma_start(out_2[0, 4 * q : 4 * q + 4, :].bitcast(I32), oq_s[32 * q : 32 * q + 4, :].bitcast(I32))

@@ -19,6 +19,7 @@ P = 128
 PACK = 4
 HALF = S // 2
 ORDER = (0, 1, 2, 3)
+ORDER2 = (0, 2, 1, 3)
 
 
 def tile_picked_mixinkgatelift_none_po_kernel(
@@ -106,8 +107,7 @@ def tile_picked_mixinkgatelift_none_po_kernel(
         nc.vector.memset(warm[:], 0.0)
         nc.scalar.activation(warm2[:], warm[:], ACT.Sigmoid)
 
-        y_ps = [psum.tile([P, S], F32, name=f"y_ps{t}") for t in range(PACK)]
-        h_ps = [psum.tile([P, S], F32, name=f"h_ps{t}") for t in range(PACK)]
+        y_ps = [psum.tile([P, S], F32, name=f"y_ps{t}", tag=f"bank{t}") for t in range(PACK)]
         for t in ORDER:
             cols = slice(t * P, (t + 1) * P)
             nc.tensor.matmul_mx(
@@ -150,7 +150,7 @@ def tile_picked_mixinkgatelift_none_po_kernel(
         z_pairs = pair_tiles("z")
         part = W // 2
         for t in ORDER:
-            if t == 3:
+            if t >= 2:
                 nc.vector.tensor_copy(ys[t][:], y_ps[t][:])
             else:
                 nc.scalar.copy(ys[t][:], y_ps[t][:])
@@ -160,62 +160,68 @@ def tile_picked_mixinkgatelift_none_po_kernel(
                     ys[t][:].indirect(n2_t[:, i * part // 16 : (i + 1) * part // 16]),
                     ACT.Sigmoid,
                 )
-        nc.scalar.activation(olds[3][:], ys[3][:].indirect(n1_t[:]), ACT.Copy)
 
         for t in ORDER:
-            if t in (1, 2):
+            if t < 2:
                 nc.vector.tensor_tensor(olds[t][:], ys[t][:].indirect(n1_t[:]), gates[t][:], ALU.mult)
                 nc.scalar.activation(ys[t][:].indirect(n1_t[:]), olds[t][:], ACT.Copy)
             else:
-                if t == 0:
-                    nc.vector.tensor_copy(olds[t][:], ys[t][:].indirect(n1_t[:]))
+                nc.vector.tensor_copy(olds[t][:], ys[t][:].indirect(n1_t[:]))
                 nc.vector.tensor_tensor(ys[t][:].indirect(n1_t[:]), olds[t][:], gates[t][:], ALU.mult)
 
         w3 = deal("w3", w3_raw, I32)
         w2 = deal("w2", w2_raw, I32)
         w23s = deal("w23s", w23s_raw, U8)
-        for t in range(PACK):
+        whole, left, right = slice(0, S), slice(0, HALF), slice(HALF, S)
+        parts = [(0, left, "bank0"), (0, right, "bank4")] + [(t, whole, f"bank{4 + t}") for t in ORDER2[1:]]
+        h_ps = [
+            psum.tile([P, side.stop - side.start], F32, name=f"h_ps{n}", tag=tag)
+            for n, (t, side, tag) in enumerate(parts)
+        ]
+        for n, (t, side, tag) in enumerate(parts):
             cols = slice(t * P, (t + 1) * P)
             nc.tensor.matmul_mx(
-                out=h_ps[t][:], lhsT=w3[:, cols].bitcast(FP8X4), lhsT_scale=w23s[4:P, cols],
-                rhs=xb[:].bitcast(FP8X4), rhs_scale=xb_s[:], start=True, stop=False,
+                out=h_ps[n][:], lhsT=w3[:, cols].bitcast(FP8X4), lhsT_scale=w23s[4:P, cols],
+                rhs=xb[:, side].bitcast(FP8X4), rhs_scale=xb_s[:, side], start=True, stop=False,
             )
         for t in ORDER:
-            round_rows(nc.vector, z_pairs, t, ys[t], gn_t[:, t : t + 1])
+            round_rows(nc.scalar if t < 2 else nc.vector, z_pairs, t, ys[t], gn_t[:, t : t + 1])
         zq, zq_s = quantise("z", z_pairs)
-        for t in range(PACK):
+        for n, (t, side, tag) in enumerate(parts):
             cols = slice(t * P, (t + 1) * P)
-            sides = [slice(0, HALF), slice(HALF, S)] if t == 0 else [slice(0, S)]
-            for side in sides:
-                nc.tensor.matmul_mx(
-                    out=h_ps[t][:, side], lhsT=w2[:, cols].bitcast(FP8X4), lhsT_scale=w23s[:, cols],
-                    rhs=zq[:, side].bitcast(FP8X4), rhs_scale=zq_s[:, side], start=False, stop=(side.stop == S),
-                )
+            nc.tensor.matmul_mx(
+                out=h_ps[n][:], lhsT=w2[:, cols].bitcast(FP8X4), lhsT_scale=w23s[:, cols],
+                rhs=zq[:, side].bitcast(FP8X4), rhs_scale=zq_s[:, side], start=False, stop=True,
+            )
 
         out_rows = out_0.rearrange("(p t) c -> t p c", t=PACK)
         o_pairs = pair_tiles("o")
         outs = [sb(f"o{t}", [P, S], F32) for t in range(PACK)]
         tops = [sb(f"top{t}", [P, U], F32) for t in range(PACK)]
-        for t in range(PACK):
+        for t in ORDER2:
             h = sb(f"h{t}", [P, S], F32)
             neg_a = sb(f"neg_a{t}", [P, U], F32)
             b = sb(f"b{t}", [P, U], F32)
-            if t == 1:
-                nc.vector.tensor_copy(h[:], h_ps[t][:])
-            else:
-                nc.scalar.copy(h[:], h_ps[t][:])
+            for n, (row, side, tag) in enumerate(parts):
+                if row == t and side == right:
+                    nc.vector.tensor_copy(h[:, side], h_ps[n][:])
+                elif row == t:
+                    nc.scalar.copy(h[:, side], h_ps[n][:])
             nc.scalar.activation(neg_a[:], h[:].indirect(n3_t[:]), ACT.Copy, scale=-1.0)
-            if t >= 2:
+            if t == 1:
                 nc.scalar.activation(b[:], h[:].indirect(n4_t[:]), ACT.Copy)
             else:
                 nc.vector.tensor_copy(b[:], h[:].indirect(n4_t[:]))
             nc.vector.scalar_tensor_tensor(tops[t][:], neg_a[:], -0.5, b[:], ALU.mult, ALU.max)
             nc.vector.tensor_tensor(outs[t][:].indirect(n3_t[:]), b[:], neg_a[:], ALU.add)
-        for t in range(PACK):
-            nc.scalar.activation(outs[t][:].indirect(n4_t[:]), tops[t][:], ACT.Copy)
+        for t in ORDER2:
+            if t == ORDER2[-1]:
+                nc.vector.tensor_copy(outs[t][:].indirect(n4_t[:]), tops[t][:])
+            else:
+                nc.scalar.activation(outs[t][:].indirect(n4_t[:]), tops[t][:], ACT.Copy)
             nc.sync.dma_start(out_rows[t], outs[t][:])
-        for t in range(PACK):
-            round_rows(nc.vector, o_pairs, t, outs[t], 1.0)
+        for t in ORDER2:
+            round_rows(nc.scalar if t < 2 else nc.vector, o_pairs, t, outs[t], 1.0)
         oq, oq_s = quantise("o", o_pairs)
         words_out = out_1[0].rearrange("p c r -> p (c r)").bitcast(I32)
         for i in range(2):

from contextlib import ExitStack

import concourse.mybir as mybir

K, T, S, N, H, W, U = 512, 2048, 512, 512, 512, 384, 256
FLOPS = 3 * 2 * 512 * 512 * 512

F32 = mybir.dt.float32
BF16 = mybir.dt.bfloat16
I32 = mybir.dt.int32
U32 = mybir.dt.uint32
U16 = mybir.dt.uint16
U8 = mybir.dt.uint8
FP8X4 = mybir.dt.float8_e4m3fn_x4
ALU = mybir.AluOpType
ACT = mybir.ActivationFunctionType

P = 128
PACK = 4
HALF = S // 2
ORDER = (0, 1, 2, 3)
ORDER2 = (0, 2, 1, 3)


def tile_picked_mixinkgatelift_none_po_kernel(
    tc, x_words, x_scales, w1_words, w1_scales, gn, w2_words, w2_scales, w3_words, w3_scales,
    offs, n1, n2, two, n3, n4, out_0, out_1, out_2,
):
    nc = tc.nc
    with ExitStack() as ctx:
        lists = ctx.enter_context(tc.tile_pool(name="lists", bufs=1))
        keep = ctx.enter_context(tc.tile_pool(name="keep", bufs=1))
        psum = ctx.enter_context(tc.psum_pool(name="psum", bufs=1))

        def sb(name, shape, dtype, tag=None):
            return keep.tile(shape, dtype, name=name, tag=tag or name, align_bytes=64)

        def load_list(name, src):
            tile = lists.tile(list(src.shape), U16, name=name)
            nc.sync.dma_start(tile[:], src)
            return tile

        def load_words(name, src, queue, tag=None):
            tile = sb(name, [P, src.shape[2]], U32, tag)
            queue.dma_start(tile[:].bitcast(I32), src[0].rearrange("p c r -> p (c r)").bitcast(I32))
            return tile

        def load_scales(tile, first, src, queue):
            for q in range(4):
                queue.dma_start(
                    tile[32 * q + first : 32 * q + first + 4, :].bitcast(I32),
                    src[0, 4 * q : 4 * q + 4, :].bitcast(I32),
                )

        def deal(name, src, dtype, tag=None):
            run = 4 if dtype == I32 else 16
            tile = sb(name, [P, 512], src.dtype, tag)
            nc.vector.tensor_copy(
                tile[:].bitcast(dtype).rearrange("p (t b m) -> p b t m", t=PACK, m=run),
                src[:].bitcast(dtype).rearrange("p (b m t) -> p b t m", t=PACK, m=run),
            )
            return tile

        def gather_tokens(name, idx, tag=None):
            words = sb(name + "_words", [P, S], U32, tag)
            scales = sb(name + "_scales", [P, S], U8)
            nc.vector.tensor_copy(scales[:], xs[:].indirect(idx[:]))
            nc.vector.tensor_copy(words[:], xw[:].indirect(idx[:]))
            return words, scales

        def load_repeated(tile, src, q, queue):
            rows = src[0, 4 * q : 4 * q + 4, :].bitcast(I32)
            queue.dma_start(
                tile[32 * q : 32 * q + 32, :].bitcast(I32),
                rows.unsqueeze(0).to_broadcast([8, 4, rows.shape[1]]),
            )

        xs = sb("xs", [P, T], U8)
        w1s_raw = sb("w1s_raw", [P, H], U8, "w1s_raw_then_w1")
        w23s_raw = sb("w23s_raw", [P, N], U8)
        nc.vector.memset(w23s_raw[:].bitcast(I32), 0)

        for q in range(4):
            load_repeated(xs, x_scales, q, nc.sync if q == 0 else nc.scalar)
        offs_t = load_list("offs_t", offs)
        two_t = load_list("two_t", two)
        xw = load_words("xw", x_words, nc.sync)
        for q in range(4):
            load_repeated(w1s_raw, w1_scales, q, nc.sync)
        w1_raw = load_words("w1_raw", w1_words, nc.sync, "w1_raw_then_xb")
        n2_t = load_list("n2_t", n2)
        n1_t = load_list("n1_t", n1)
        w3_raw = load_words("w3_raw", w3_words, nc.sync)
        w2_raw = load_words("w2_raw", w2_words, nc.sync)
        load_scales(w23s_raw, 0, w2_scales, nc.sync)
        load_scales(w23s_raw, 4, w3_scales, nc.sync)
        gn_t = sb("gn_t", [P, PACK], F32)
        nc.sync.dma_start(gn_t[:], gn.rearrange("(p t) o -> p (t o)", t=PACK))
        n3_t = load_list("n3_t", n3)
        n4_t = load_list("n4_t", n4)

        xa, xa_s = gather_tokens("xa", offs_t)
        w1s = deal("w1s", w1s_raw, U8)
        w1 = deal("w1", w1_raw, I32, "w1s_raw_then_w1")
        warm = sb("warm", [P, 1], F32)
        warm2 = sb("warm2", [P, 1], F32)
        nc.vector.memset(warm[:], 0.0)
        nc.scalar.activation(warm2[:], warm[:], ACT.Sigmoid)

        y_ps = [psum.tile([P, S], F32, name=f"y_ps{t}", tag=f"bank{t}") for t in range(PACK)]
        for t in ORDER:
            cols = slice(t * P, (t + 1) * P)
            nc.tensor.matmul_mx(
                out=y_ps[t][:], lhsT=w1[:, cols].bitcast(FP8X4), lhsT_scale=w1s[:, cols],
                rhs=xa[:].bitcast(FP8X4), rhs_scale=xa_s[:], start=True, stop=True,
            )
        xb, xb_s = gather_tokens("xb", two_t, "w1_raw_then_xb")

        def pair_tiles(name):
            return [sb(f"{name}_pairs{i}", [P, 2, HALF, 2], BF16) for i in range(2)]

        def round_rows(engine, pairs, t, src, scale):
            for i in range(2):
                dst = pairs[i][:, t // 2, :, t % 2]
                cols = src[:, i * HALF : (i + 1) * HALF]
                if engine is nc.scalar:
                    nc.scalar.activation(dst, cols, ACT.Copy, scale=scale)
                else:
                    nc.vector.tensor_scalar(dst, cols, scale, None, ALU.mult)

        def quantise(name, pairs):
            grouped = [sb(f"{name}_grouped{i}", [P, HALF, 2], I32) for i in range(2)]
            words = sb(name + "_words", [P, S], U32)
            scales = sb(name + "_scales", [P, S], U8)
            for i in range(2):
                nc.vector.tensor_copy(
                    grouped[i][:],
                    pairs[i][:].rearrange("p u c e -> p u (c e)").bitcast(I32).rearrange("p u c -> p c u"),
                )
            for i in range(2):
                nc.vector.quantize_mx(
                    out=words[:, i * HALF : (i + 1) * HALF].bitcast(FP8X4), scales=scales[:, i * HALF : (i + 1) * HALF],
                    in_=grouped[i][:].rearrange("p c u -> p (c u)").bitcast(BF16),
                )
            return words, scales

        ys = [sb(f"y{t}", [P, S], F32) for t in range(PACK)]
        gates = [sb(f"gate{t}", [P, W], F32) for t in range(PACK)]
        olds = [sb(f"old{t}", [P, W], F32) for t in range(PACK)]
        z_pairs = pair_tiles("z")
        part = W // 2
        for t in ORDER:
            if t >= 2:
                nc.vector.tensor_copy(ys[t][:], y_ps[t][:])
            else:
                nc.scalar.copy(ys[t][:], y_ps[t][:])
            for i in range(2):
                nc.scalar.activation(
                    gates[t][:, i * part : (i + 1) * part],
                    ys[t][:].indirect(n2_t[:, i * part // 16 : (i + 1) * part // 16]),
                    ACT.Sigmoid,
                )

        for t in ORDER:
            if t < 2:
                nc.vector.tensor_tensor(olds[t][:], ys[t][:].indirect(n1_t[:]), gates[t][:], ALU.mult)
                nc.scalar.activation(ys[t][:].indirect(n1_t[:]), olds[t][:], ACT.Copy)
            else:
                nc.vector.tensor_copy(olds[t][:], ys[t][:].indirect(n1_t[:]))
                nc.vector.tensor_tensor(ys[t][:].indirect(n1_t[:]), olds[t][:], gates[t][:], ALU.mult)

        w3 = deal("w3", w3_raw, I32)
        w2 = deal("w2", w2_raw, I32)
        w23s = deal("w23s", w23s_raw, U8)
        whole, left, right = slice(0, S), slice(0, HALF), slice(HALF, S)
        parts = [(0, left, "bank0"), (0, right, "bank4")] + [(t, whole, f"bank{4 + t}") for t in ORDER2[1:]]
        h_ps = [
            psum.tile([P, side.stop - side.start], F32, name=f"h_ps{n}", tag=tag)
            for n, (t, side, tag) in enumerate(parts)
        ]
        for n, (t, side, tag) in enumerate(parts):
            cols = slice(t * P, (t + 1) * P)
            nc.tensor.matmul_mx(
                out=h_ps[n][:], lhsT=w3[:, cols].bitcast(FP8X4), lhsT_scale=w23s[4:P, cols],
                rhs=xb[:, side].bitcast(FP8X4), rhs_scale=xb_s[:, side], start=True, stop=False,
            )
        for t in ORDER:
            round_rows(nc.scalar if t < 2 else nc.vector, z_pairs, t, ys[t], gn_t[:, t : t + 1])
        zq, zq_s = quantise("z", z_pairs)
        for n, (t, side, tag) in enumerate(parts):
            cols = slice(t * P, (t + 1) * P)
            nc.tensor.matmul_mx(
                out=h_ps[n][:], lhsT=w2[:, cols].bitcast(FP8X4), lhsT_scale=w23s[:, cols],
                rhs=zq[:, side].bitcast(FP8X4), rhs_scale=zq_s[:, side], start=False, stop=True,
            )

        out_rows = out_0.rearrange("(p t) c -> t p c", t=PACK)
        o_pairs = pair_tiles("o")
        outs = [sb(f"o{t}", [P, S], F32) for t in range(PACK)]
        tops = [sb(f"top{t}", [P, U], F32) for t in range(PACK)]
        for t in ORDER2:
            h = sb(f"h{t}", [P, S], F32)
            neg_a = sb(f"neg_a{t}", [P, U], F32)
            b = sb(f"b{t}", [P, U], F32)
            for n, (row, side, tag) in enumerate(parts):
                if row == t and side == right:
                    nc.vector.tensor_copy(h[:, side], h_ps[n][:])
                elif row == t:
                    nc.scalar.copy(h[:, side], h_ps[n][:])
            nc.scalar.activation(neg_a[:], h[:].indirect(n3_t[:]), ACT.Copy, scale=-1.0)
            if t == 1:
                nc.scalar.activation(b[:], h[:].indirect(n4_t[:]), ACT.Copy)
            else:
                nc.vector.tensor_copy(b[:], h[:].indirect(n4_t[:]))
            nc.vector.scalar_tensor_tensor(tops[t][:], neg_a[:], -0.5, b[:], ALU.mult, ALU.max)
            nc.vector.tensor_tensor(outs[t][:].indirect(n3_t[:]), b[:], neg_a[:], ALU.add)
        for t in ORDER2:
            if t == ORDER2[-1]:
                nc.vector.tensor_copy(outs[t][:].indirect(n4_t[:]), tops[t][:])
            else:
                nc.scalar.activation(outs[t][:].indirect(n4_t[:]), tops[t][:], ACT.Copy)
            nc.sync.dma_start(out_rows[t], outs[t][:])
        for t in ORDER2:
            round_rows(nc.scalar if t < 2 else nc.vector, o_pairs, t, outs[t], 1.0)
        oq, oq_s = quantise("o", o_pairs)
        words_out = out_1[0].rearrange("p c r -> p (c r)").bitcast(I32)
        for i in range(2):
            nc.sync.dma_start(words_out[:, i * HALF : (i + 1) * HALF], oq[:, i * HALF : (i + 1) * HALF].bitcast(I32))
        for q in range(4):
            queue = nc.scalar if q % 2 == 0 else nc.sync
            queue.dma_start(out_2[0, 4 * q : 4 * q + 4, :].bitcast(I32), oq_s[32 * q : 32 * q + 4, :].bitcast(I32))
